import numpy as np
import ml_dtypes


def mxq(x, axis, fmt="e4m3"):
    dtype, down = {"e4m3": (ml_dtypes.float8_e4m3fn, 7), "e5m2": (ml_dtypes.float8_e5m2, 14)}[fmt]
    v = np.moveaxis(np.asarray(x, np.float32).astype(ml_dtypes.bfloat16).astype(np.float64), axis, -1)
    blocks = v.reshape(v.shape[:-1] + (-1, 32))
    amax = np.abs(blocks).max(-1, keepdims=True)
    byte = np.maximum(np.where(amax > 0, np.frexp(amax)[1] - 1 + 127, 0) - down, 1)
    scale = np.exp2(byte - 127.0)
    codes = (blocks / scale).astype(np.float32).astype(dtype).astype(np.float64)
    return np.moveaxis((codes * scale).reshape(v.shape), -1, axis)


WIDE = False


def mx_kscale(k):
    if not WIDE:
        return np.ones(k)
    levels = np.array([10, -10, 5, -5, 0])
    if k % 512:
        return np.exp2(np.random.permutation(np.resize(levels, k // 32))).repeat(32)
    a = np.empty((k // 512, 16))
    for p in range(k // 512):
        a[p, :8] = np.random.permutation(np.resize(levels, 8))
        for g in range(8):
            far = levels[np.abs(levels - a[p, g]) >= 10]
            a[p, g + 8] = far[np.random.randint(len(far))]
    return np.exp2(a.ravel()).repeat(32)


def f64(x):
    return np.asarray(x).astype(np.float64)


def striped(idx):
    return np.tile(idx.reshape(-1, 16).T, (8, 1)).astype(np.uint16)


def unstriped(offs):
    return offs[:16].T.reshape(-1).astype(np.int64)


def pack_weight(w):
    k, n = w.shape
    w = f64(np.asarray(w, np.float32).astype(ml_dtypes.bfloat16)).reshape(k // 32, 32, n)
    amax = np.abs(w).max(1)
    byte = np.clip(np.where(amax > 0, np.frexp(amax)[1] - 1 + 127 - 7, 1), 1, 254)
    scaled = (w * np.exp2(127.0 - byte)[:, None, :]).reshape(k, n).astype(np.float32)
    words = np.ascontiguousarray(scaled.reshape(k // 512, 128, 4, n).transpose(0, 1, 3, 2)).astype(ml_dtypes.float8_e4m3fn).view(np.uint8)
    return words, np.ascontiguousarray(byte.astype(np.uint8).reshape(k // 512, 16, n))


def unpack_weight(words, scales):
    g, p, n, _ = words.shape
    vals = np.ascontiguousarray(words).view(ml_dtypes.float8_e4m3fn).astype(np.float64) * np.repeat(np.exp2(scales.astype(np.float64) - 127.0), 8, axis=1)[..., None]
    return vals.transpose(0, 1, 3, 2).reshape(g * 512, n)


def planes(y):
    n, m = y.shape
    v = y.astype(np.float32).astype(ml_dtypes.bfloat16).astype(np.float64).reshape(n // 32, 32, m)
    top = np.abs(v).max(1)
    byte = np.clip(np.where(top > 0, np.frexp(top)[1] - 1 + 127 - 7, 1), 1, 254)
    codes = (v * np.exp2(127.0 - byte)[:, None, :]).reshape(n, m).astype(np.float32).astype(ml_dtypes.float8_e4m3fn).view(np.uint8)
    words = codes.reshape(n // 512, 128, 4, m).transpose(0, 1, 3, 2)
    return np.ascontiguousarray(words), np.ascontiguousarray(byte.astype(np.uint8).reshape(n // 512, 16, m))


K, T, S, N = 512, 1024, 512, 512


def setup_inputs():
    n = np.random.standard_normal
    s = mx_kscale(K)[:, None]
    packed_xT = pack_weight(n((K, T)) * s)
    return {
        "x_words": packed_xT[0],
        "x_scales": packed_xT[1],
        "eT": (n((K, S)) * s).astype(np.float32),
        "w1": (n((K, N)) / np.sqrt(2 * K) / s).astype(np.float32),
        "w2": (n((K, N)) / np.sqrt(2 * K) / s).astype(np.float32),
        "w3": (n((K, N)) / np.sqrt(2 * K) / s).astype(np.float32),
        "w4": (n((K, N)) / np.sqrt(2 * K) / s).astype(np.float32),
        "dec": (n((N, S))).astype(np.float32),
        "offs": striped(np.random.permutation(T)[:S]),
    }


def reference(x_words, x_scales, eT, w1, w2, w3, w4, dec, offs):
    eTq = mxq(f64(eT), 0, "e4m3")
    xq = unpack_weight(x_words, x_scales)[:, unstriped(offs)]
    g = np.tanh(mxq(f64(w1), 0, "e4m3").T @ eTq + mxq(f64(w2), 0, "e4m3").T @ xq)
    h = mxq(f64(w3), 0, "e4m3").T @ eTq + mxq(f64(w4), 0, "e4m3").T @ xq
    out_0 = f64(dec) * g + h
    return (out_0,) + planes(out_0)

@@ -1,0 +1,174 @@
+from contextlib import ExitStack
+
+import concourse.mybir as mybir
+
+F32 = mybir.dt.float32
+BF16 = mybir.dt.bfloat16
+I32 = mybir.dt.int32
+U32 = mybir.dt.uint32
+U16 = mybir.dt.uint16
+U8 = mybir.dt.uint8
+FP8X4 = mybir.dt.float8_e4m3fn_x4
+TANH = mybir.ActivationFunctionType.Tanh
+MULT = mybir.AluOpType.mult
+ADD = mybir.AluOpType.add
+
+P = 128
+PACK = 4
+K = 512
+ROWS = 512
+COLS = 512
+TABLE = 1024
+HALF = COLS // 2
+FLOPS = 4 * 2 * K * ROWS * COLS
+
+
+def tile_picked_zcft_tanh_po_kernel(
+    tc, x_words, x_scales, eT, w1, w2, w3, w4, dec, offs, out_0, out_1, out_2
+):
+    nc = tc.nc
+    with ExitStack() as ctx:
+        keep = ctx.enter_context(tc.tile_pool(name="keep", bufs=1))
+        psum = ctx.enter_context(tc.psum_pool(name="psum", bufs=1))
+
+        def sb(name, shape, dtype):
+            return keep.tile(shape, dtype, name=name, align_bytes=64)
+
+        def vector_copy(out, in_):
+            nc.vector.tensor_copy(out=out, in_=in_)
+
+        def scalar_copy(out, in_):
+            nc.scalar.copy(out=out, in_=in_)
+
+        offsets = keep.tile([P, COLS // 16], U16, name="offsets")
+        nc.sync.dma_start(offsets[:], offs)
+
+        warm = sb("warm", [P, 1], F32)
+        warm_out = sb("warm_out", [P, 1], F32)
+        nc.gpsimd.memset(warm[:], 0.0)
+        nc.scalar.activation(out=warm_out[:], in_=warm[:], func=TANH)
+
+        table_words = sb("table_words", [P, TABLE], U32)
+        nc.sync.dma_start(
+            out=table_words[:].bitcast(I32),
+            in_=x_words[0].rearrange("p c r -> p (c r)").bitcast(I32),
+        )
+        table_scales = sb("table_scales", [P, TABLE], U8)
+        nc.vector.memset(table_scales[:].bitcast(I32), 0)
+        for q in range(4):
+            nc.sync.dma_start(
+                out=table_scales[32 * q : 32 * q + 4, :].bitcast(I32),
+                in_=x_scales[0, 4 * q : 4 * q + 4, :].bitcast(I32),
+            )
+
+        def load(name, src):
+            raw = sb(name, [P, PACK, src.shape[1]], F32)
+            nc.sync.dma_start(out=raw[:], in_=src.rearrange("(p j) c -> p j c", j=PACK))
+            return raw
+
+        e_raw = load("e_raw", eT)
+        w2_raw = load("w2_raw", w2)
+        w1_raw = load("w1_raw", w1)
+        w3_raw = load("w3_raw", w3)
+        w4_raw = load("w4_raw", w4)
+        dec_rows = dec.rearrange("(p t) c -> p t c", t=PACK)
+        dec_sb = []
+        for u in range(2):
+            d = sb("dec%d" % u, [P, 2, COLS], F32)
+            nc.sync.dma_start(out=d[:], in_=dec_rows[:, 2 * u : 2 * u + 2, :])
+            dec_sb.append(d)
+
+        x_codes = sb("x_codes", [P, COLS], U32)
+        x_plane = sb("x_plane", [P, COLS], U8)
+        nc.vector.tensor_copy(out=x_codes[:], in_=table_words[:].indirect(offsets[:]))
+        nc.vector.tensor_copy(out=x_plane[:], in_=table_scales[:].indirect(offsets[:]))
+
+        def interleave(copy, grouped, rows):
+            copy(
+                grouped.rearrange("p (c i) t -> p c t i", i=4),
+                rows.rearrange("p t (c i) -> p c t i", i=4),
+            )
+
+        def quantize(codes, plane, grouped):
+            nc.vector.quantize_mx(out=codes.bitcast(FP8X4), scales=plane, in_=grouped)
+
+        e_codes = sb("e_codes", [P, COLS], U32)
+        e_plane = sb("e_plane", [P, COLS], U8)
+        e_bf = [sb("e_bf%d" % h, [P, HALF, PACK], BF16) for h in range(2)]
+        for h, copy in enumerate((vector_copy, scalar_copy)):
+            interleave(copy, e_bf[h][:], e_raw[:, :, h * HALF : (h + 1) * HALF])
+        for h in range(2):
+            cols = slice(h * HALF, (h + 1) * HALF)
+            quantize(e_codes[:, cols], e_plane[:, cols], e_bf[h][:].rearrange("p c t -> p (c t)"))
+
+        def weight_pass(name, raw, copies, banks, rhs_codes, rhs_plane, first):
+            dealt = raw[:].rearrange("p j (m t) -> p m j t", t=PACK)
+            bf = [sb("%s_bf%d" % (name, u), [P, 2, P, PACK], BF16) for u in range(2)]
+            for u in range(2):
+                copies[u](bf[u][:].rearrange("p t m j -> p m j t"), dealt[:, :, :, 2 * u : 2 * u + 2])
+            for u in range(2):
+                codes = sb("%s_codes%d" % (name, u), [P, 2 * P], U32)
+                plane = sb("%s_plane%d" % (name, u), [P, 2 * P], U8)
+                quantize(codes[:], plane[:], bf[u][:].rearrange("p t m j -> p (t m j)"))
+                for s in range(2):
+                    nc.tensor.matmul_mx(
+                        out=banks[2 * u + s][:],
+                        lhsT=codes[:, s * P : (s + 1) * P].bitcast(FP8X4),
+                        lhsT_scale=plane[:, s * P : (s + 1) * P],
+                        rhs=rhs_codes[:].bitcast(FP8X4),
+                        rhs_scale=rhs_plane[:],
+                        start=first,
+                        stop=not first,
+                    )
+
+        g_banks = [psum.tile([P, COLS], F32, name="g_bank%d" % t) for t in range(PACK)]
+        h_banks = [psum.tile([P, COLS], F32, name="h_bank%d" % t) for t in range(PACK)]
+        shared = (vector_copy, scalar_copy)
+        weight_pass("w2", w2_raw, shared, g_banks, x_codes, x_plane, True)
+        weight_pass("w1", w1_raw, shared, g_banks, e_codes, e_plane, False)
+        g_sb = [sb("g%d" % u, [P, 2, COLS], F32) for u in range(2)]
+        for t in range(PACK):
+            nc.scalar.activation(out=g_sb[t // 2][:, t % 2, :], in_=g_banks[t][:], func=TANH)
+        weight_pass("w3", w3_raw, (vector_copy, vector_copy), h_banks, e_codes, e_plane, True)
+        weight_pass("w4", w4_raw, shared, h_banks, x_codes, x_plane, False)
+
+        chunks = ((0, 256, scalar_copy), (256, 128, scalar_copy), (384, 128, vector_copy))
+        scaled = [[sb("scaled%d_%d" % (h, u), [P, 2, HALF], F32) for u in range(2)] for h in range(2)]
+        y_codes = sb("y_codes", [P, COLS], U32)
+        y_plane = sb("y_plane", [P, COLS], U8)
+        out_rows = out_0.rearrange("(p t) c -> p t c", t=PACK)
+        out_words = out_1[0].rearrange("p c r -> p (c r)").bitcast(I32)
+
+        def scale(h, u):
+            cols = slice(h * HALF, (h + 1) * HALF)
+            nc.vector.tensor_tensor(
+                out=scaled[h][u][:], in0=dec_sb[u][:, :, cols], in1=g_sb[u][:, :, cols], op=MULT
+            )
+
+        y_bf = []
+        for c0, width, copy in chunks:
+            h, off = divmod(c0, HALF)
+            y = sb("y%d" % c0, [P, PACK, width], F32)
+            for t in range(PACK):
+                if off == 0 and t % 2 == 0:
+                    scale(h, t // 2)
+                nc.vector.tensor_tensor(
+                    out=y[:, t, :],
+                    in0=h_banks[t][:, c0 : c0 + width],
+                    in1=scaled[h][t // 2][:, t % 2, off : off + width],
+                    op=ADD,
+                )
+            nc.sync.dma_start(out=out_rows[:, :, c0 : c0 + width], in_=y[:])
+            bf = sb("y_bf%d" % c0, [P, width, PACK], BF16)
+            interleave(copy, bf[:], y[:])
+            y_bf.append(bf)
+        for (c0, width, copy), bf in zip(chunks, y_bf):
+            cols = slice(c0, c0 + width)
+            quantize(y_codes[:, cols], y_plane[:, cols], bf[:].rearrange("p c t -> p (c t)"))
+        nc.sync.dma_start(out=out_words, in_=y_codes[:].bitcast(I32))
+        for q in range(4):
+            eng = nc.scalar if q % 2 == 0 else nc.sync
+            eng.dma_start(
+                out=out_2[0, 4 * q : 4 * q + 4, :].bitcast(I32),
+                in_=y_plane[32 * q : 32 * q + 4, :].bitcast(I32),
+            )

@@ -40,26 +40,24 @@ def tile_picked_zcft_tanh_po_kernel(
         def scalar_copy(out, in_):
             nc.scalar.copy(out=out, in_=in_)
 
-        offsets = keep.tile([P, COLS // 16], U16, name="offsets")
-        nc.sync.dma_start(offsets[:], offs)
-
-        warm = sb("warm", [P, 1], F32)
-        warm_out = sb("warm_out", [P, 1], F32)
-        nc.gpsimd.memset(warm[:], 0.0)
-        nc.scalar.activation(out=warm_out[:], in_=warm[:], func=TANH)
-
         table_words = sb("table_words", [P, TABLE], U32)
         nc.sync.dma_start(
             out=table_words[:].bitcast(I32),
             in_=x_words[0].rearrange("p c r -> p (c r)").bitcast(I32),
         )
+        offsets = keep.tile([P, COLS // 16], U16, name="offsets")
+        nc.sync.dma_start(offsets[:], offs)
+
+        scale_rows = sb("scale_rows", [P, TABLE], U8)
         table_scales = sb("table_scales", [P, TABLE], U8)
         nc.vector.memset(table_scales[:].bitcast(I32), 0)
         for q in range(4):
+            live = slice(32 * q, 32 * q + 4)
             nc.sync.dma_start(
-                out=table_scales[32 * q : 32 * q + 4, :].bitcast(I32),
+                out=scale_rows[live, :].bitcast(I32),
                 in_=x_scales[0, 4 * q : 4 * q + 4, :].bitcast(I32),
             )
+            nc.vector.tensor_copy(out=table_scales[live, :].bitcast(I32), in_=scale_rows[live, :].bitcast(I32))
 
         def load(name, src):
             raw = sb(name, [P, PACK, src.shape[1]], F32)
@@ -132,8 +130,9 @@ def tile_picked_zcft_tanh_po_kernel(
         weight_pass("w3", w3_raw, (vector_copy, vector_copy), h_banks, e_codes, e_plane, True)
         weight_pass("w4", w4_raw, shared, h_banks, x_codes, x_plane, False)
 
-        chunks = ((0, 256, scalar_copy), (256, 128, scalar_copy), (384, 128, vector_copy))
         scaled = [[sb("scaled%d_%d" % (h, u), [P, 2, HALF], F32) for u in range(2)] for h in range(2)]
+        y = [sb("y%d" % h, [P, PACK, HALF], F32) for h in range(2)]
+        y_bf = [sb("y_bf%d" % h, [P, HALF, PACK], BF16) for h in range(2)]
         y_codes = sb("y_codes", [P, COLS], U32)
         y_plane = sb("y_plane", [P, COLS], U8)
         out_rows = out_0.rearrange("(p t) c -> p t c", t=PACK)
@@ -145,27 +144,33 @@ def tile_picked_zcft_tanh_po_kernel(
                 out=scaled[h][u][:], in0=dec_sb[u][:, :, cols], in1=g_sb[u][:, :, cols], op=MULT
             )
 
-        y_bf = []
-        for c0, width, copy in chunks:
-            h, off = divmod(c0, HALF)
-            y = sb("y%d" % c0, [P, PACK, width], F32)
-            for t in range(PACK):
-                if off == 0 and t % 2 == 0:
-                    scale(h, t // 2)
+        def add(h, u):
+            cols = slice(h * HALF, (h + 1) * HALF)
+            rows = slice(2 * u, 2 * u + 2)
+            for s in range(2):
                 nc.vector.tensor_tensor(
-                    out=y[:, t, :],
-                    in0=h_banks[t][:, c0 : c0 + width],
-                    in1=scaled[h][t // 2][:, t % 2, off : off + width],
-                    op=ADD,
+                    out=y[h][:, 2 * u + s, :], in0=h_banks[2 * u + s][:, cols], in1=scaled[h][u][:, s, :], op=ADD
                 )
-            nc.sync.dma_start(out=out_rows[:, :, c0 : c0 + width], in_=y[:])
-            bf = sb("y_bf%d" % c0, [P, width, PACK], BF16)
-            interleave(copy, bf[:], y[:])
-            y_bf.append(bf)
-        for (c0, width, copy), bf in zip(chunks, y_bf):
-            cols = slice(c0, c0 + width)
-            quantize(y_codes[:, cols], y_plane[:, cols], bf[:].rearrange("p c t -> p (c t)"))
-        nc.sync.dma_start(out=out_words, in_=y_codes[:].bitcast(I32))
+            nc.sync.dma_start(out=out_rows[:, rows, cols], in_=y[h][:, rows, :])
+
+        def finish(h):
+            cols = slice(h * HALF, (h + 1) * HALF)
+            quantize(y_codes[:, cols], y_plane[:, cols], y_bf[h][:].rearrange("p c t -> p (c t)"))
+            nc.sync.dma_start(out=out_words[:, cols], in_=y_codes[:, cols].bitcast(I32))
+
+        scale(0, 0)
+        add(0, 0)
+        scale(0, 1)
+        scale(1, 0)
+        add(0, 1)
+        interleave(scalar_copy, y_bf[0][:], y[0][:])
+        scale(1, 1)
+        add(1, 0)
+        add(1, 1)
+        interleave(vector_copy, y_bf[1][:, 0:160, :], y[1][:, :, 0:160])
+        interleave(scalar_copy, y_bf[1][:, 160:HALF, :], y[1][:, :, 160:HALF])
+        finish(0)
+        finish(1)
         for q in range(4):
             eng = nc.scalar if q % 2 == 0 else nc.sync
             eng.dma_start(

@@ -15,11 +15,16 @@ ADD = mybir.AluOpType.add
 
 P = 128
 PACK = 4
+PAIRS = PACK // 2
+QUADRANTS = 4
 K = 512
 ROWS = 512
 COLS = 512
 TABLE = 1024
 HALF = COLS // 2
+LIST_ROWS = 16
+RUN = 4
+VECTOR_SHARE = 160
 FLOPS = 4 * 2 * K * ROWS * COLS
 
 
@@ -40,24 +45,28 @@ def tile_picked_zcft_tanh_po_kernel(
         def scalar_copy(out, in_):
             nc.scalar.copy(out=out, in_=in_)
 
+        def plane_rows(q):
+            return slice(32 * q, 32 * q + 4), slice(4 * q, 4 * q + 4)
+
+        def half(h):
+            return slice(h * HALF, (h + 1) * HALF)
+
+        def pair(u):
+            return slice(2 * u, 2 * u + 2)
+
+        offsets = keep.tile([P, COLS // LIST_ROWS], U16, name="offsets")
+        nc.sync.dma_start(offsets[:], offs)
+
         table_words = sb("table_words", [P, TABLE], U32)
         nc.sync.dma_start(
             out=table_words[:].bitcast(I32),
             in_=x_words[0].rearrange("p c r -> p (c r)").bitcast(I32),
         )
-        offsets = keep.tile([P, COLS // 16], U16, name="offsets")
-        nc.sync.dma_start(offsets[:], offs)
-
-        scale_rows = sb("scale_rows", [P, TABLE], U8)
-        table_scales = sb("table_scales", [P, TABLE], U8)
-        nc.vector.memset(table_scales[:].bitcast(I32), 0)
-        for q in range(4):
-            live = slice(32 * q, 32 * q + 4)
-            nc.sync.dma_start(
-                out=scale_rows[live, :].bitcast(I32),
-                in_=x_scales[0, 4 * q : 4 * q + 4, :].bitcast(I32),
-            )
-            nc.vector.tensor_copy(out=table_scales[live, :].bitcast(I32), in_=scale_rows[live, :].bitcast(I32))
+        table_plane = sb("table_plane", [P, TABLE], U8)
+        nc.vector.memset(table_plane[:].bitcast(I32), 0)
+        for q in range(QUADRANTS):
+            parts, rows = plane_rows(q)
+            nc.sync.dma_start(out=table_plane[parts, :].bitcast(I32), in_=x_scales[0, rows, :].bitcast(I32))
 
         def load(name, src):
             raw = sb(name, [P, PACK, src.shape[1]], F32)
@@ -71,40 +80,40 @@ def tile_picked_zcft_tanh_po_kernel(
         w4_raw = load("w4_raw", w4)
         dec_rows = dec.rearrange("(p t) c -> p t c", t=PACK)
         dec_sb = []
-        for u in range(2):
-            d = sb("dec%d" % u, [P, 2, COLS], F32)
-            nc.sync.dma_start(out=d[:], in_=dec_rows[:, 2 * u : 2 * u + 2, :])
-            dec_sb.append(d)
+        for u in range(PAIRS):
+            dec_pair = sb("dec%d" % u, [P, 2, COLS], F32)
+            nc.sync.dma_start(out=dec_pair[:], in_=dec_rows[:, pair(u), :])
+            dec_sb.append(dec_pair)
 
         x_codes = sb("x_codes", [P, COLS], U32)
         x_plane = sb("x_plane", [P, COLS], U8)
         nc.vector.tensor_copy(out=x_codes[:], in_=table_words[:].indirect(offsets[:]))
-        nc.vector.tensor_copy(out=x_plane[:], in_=table_scales[:].indirect(offsets[:]))
+        nc.vector.tensor_copy(out=x_plane[:], in_=table_plane[:].indirect(offsets[:]))
 
         def interleave(copy, grouped, rows):
             copy(
-                grouped.rearrange("p (c i) t -> p c t i", i=4),
-                rows.rearrange("p t (c i) -> p c t i", i=4),
+                grouped.rearrange("p (c i) t -> p c t i", i=RUN),
+                rows.rearrange("p t (c i) -> p c t i", i=RUN),
             )
 
         def quantize(codes, plane, grouped):
             nc.vector.quantize_mx(out=codes.bitcast(FP8X4), scales=plane, in_=grouped)
 
+        shared = (vector_copy, scalar_copy)
         e_codes = sb("e_codes", [P, COLS], U32)
         e_plane = sb("e_plane", [P, COLS], U8)
         e_bf = [sb("e_bf%d" % h, [P, HALF, PACK], BF16) for h in range(2)]
-        for h, copy in enumerate((vector_copy, scalar_copy)):
-            interleave(copy, e_bf[h][:], e_raw[:, :, h * HALF : (h + 1) * HALF])
+        for h, copy in enumerate(shared):
+            interleave(copy, e_bf[h][:], e_raw[:, :, half(h)])
         for h in range(2):
-            cols = slice(h * HALF, (h + 1) * HALF)
-            quantize(e_codes[:, cols], e_plane[:, cols], e_bf[h][:].rearrange("p c t -> p (c t)"))
+            quantize(e_codes[:, half(h)], e_plane[:, half(h)], e_bf[h][:].rearrange("p c t -> p (c t)"))
 
         def weight_pass(name, raw, copies, banks, rhs_codes, rhs_plane, first):
             dealt = raw[:].rearrange("p j (m t) -> p m j t", t=PACK)
-            bf = [sb("%s_bf%d" % (name, u), [P, 2, P, PACK], BF16) for u in range(2)]
-            for u in range(2):
-                copies[u](bf[u][:].rearrange("p t m j -> p m j t"), dealt[:, :, :, 2 * u : 2 * u + 2])
-            for u in range(2):
+            bf = [sb("%s_bf%d" % (name, u), [P, 2, P, PACK], BF16) for u in range(PAIRS)]
+            for u in range(PAIRS):
+                copies[u](bf[u][:].rearrange("p t m j -> p m j t"), dealt[:, :, :, pair(u)])
+            for u in range(PAIRS):
                 codes = sb("%s_codes%d" % (name, u), [P, 2 * P], U32)
                 plane = sb("%s_plane%d" % (name, u), [P, 2 * P], U8)
                 quantize(codes[:], plane[:], bf[u][:].rearrange("p t m j -> p (t m j)"))
@@ -121,16 +130,15 @@ def tile_picked_zcft_tanh_po_kernel(
 
         g_banks = [psum.tile([P, COLS], F32, name="g_bank%d" % t) for t in range(PACK)]
         h_banks = [psum.tile([P, COLS], F32, name="h_bank%d" % t) for t in range(PACK)]
-        shared = (vector_copy, scalar_copy)
         weight_pass("w2", w2_raw, shared, g_banks, x_codes, x_plane, True)
         weight_pass("w1", w1_raw, shared, g_banks, e_codes, e_plane, False)
-        g_sb = [sb("g%d" % u, [P, 2, COLS], F32) for u in range(2)]
+        g_sb = [sb("g%d" % u, [P, 2, COLS], F32) for u in range(PAIRS)]
         for t in range(PACK):
             nc.scalar.activation(out=g_sb[t // 2][:, t % 2, :], in_=g_banks[t][:], func=TANH)
         weight_pass("w3", w3_raw, (vector_copy, vector_copy), h_banks, e_codes, e_plane, True)
         weight_pass("w4", w4_raw, shared, h_banks, x_codes, x_plane, False)
 
-        scaled = [[sb("scaled%d_%d" % (h, u), [P, 2, HALF], F32) for u in range(2)] for h in range(2)]
+        scaled = [[sb("scaled%d_%d" % (h, u), [P, 2, HALF], F32) for u in range(PAIRS)] for h in range(2)]
         y = [sb("y%d" % h, [P, PACK, HALF], F32) for h in range(2)]
         y_bf = [sb("y_bf%d" % h, [P, HALF, PACK], BF16) for h in range(2)]
         y_codes = sb("y_codes", [P, COLS], U32)
@@ -139,41 +147,35 @@ def tile_picked_zcft_tanh_po_kernel(
         out_words = out_1[0].rearrange("p c r -> p (c r)").bitcast(I32)
 
         def scale(h, u):
-            cols = slice(h * HALF, (h + 1) * HALF)
             nc.vector.tensor_tensor(
-                out=scaled[h][u][:], in0=dec_sb[u][:, :, cols], in1=g_sb[u][:, :, cols], op=MULT
+                out=scaled[h][u][:], in0=dec_sb[u][:, :, half(h)], in1=g_sb[u][:, :, half(h)], op=MULT
             )
 
-        def add(h, u):
-            cols = slice(h * HALF, (h + 1) * HALF)
-            rows = slice(2 * u, 2 * u + 2)
+        def shift(h, u):
             for s in range(2):
                 nc.vector.tensor_tensor(
-                    out=y[h][:, 2 * u + s, :], in0=h_banks[2 * u + s][:, cols], in1=scaled[h][u][:, s, :], op=ADD
+                    out=y[h][:, 2 * u + s, :], in0=h_banks[2 * u + s][:, half(h)], in1=scaled[h][u][:, s, :], op=ADD
                 )
-            nc.sync.dma_start(out=out_rows[:, rows, cols], in_=y[h][:, rows, :])
+            nc.sync.dma_start(out=out_rows[:, pair(u), half(h)], in_=y[h][:, pair(u), :])
 
         def finish(h):
-            cols = slice(h * HALF, (h + 1) * HALF)
-            quantize(y_codes[:, cols], y_plane[:, cols], y_bf[h][:].rearrange("p c t -> p (c t)"))
-            nc.sync.dma_start(out=out_words[:, cols], in_=y_codes[:, cols].bitcast(I32))
+            quantize(y_codes[:, half(h)], y_plane[:, half(h)], y_bf[h][:].rearrange("p c t -> p (c t)"))
+            nc.sync.dma_start(out=out_words[:, half(h)], in_=y_codes[:, half(h)].bitcast(I32))
 
         scale(0, 0)
-        add(0, 0)
+        shift(0, 0)
         scale(0, 1)
         scale(1, 0)
-        add(0, 1)
+        shift(0, 1)
         interleave(scalar_copy, y_bf[0][:], y[0][:])
         scale(1, 1)
-        add(1, 0)
-        add(1, 1)
-        interleave(vector_copy, y_bf[1][:, 0:160, :], y[1][:, :, 0:160])
-        interleave(scalar_copy, y_bf[1][:, 160:HALF, :], y[1][:, :, 160:HALF])
+        shift(1, 0)
+        shift(1, 1)
+        interleave(vector_copy, y_bf[1][:, 0:VECTOR_SHARE, :], y[1][:, :, 0:VECTOR_SHARE])
+        interleave(scalar_copy, y_bf[1][:, VECTOR_SHARE:HALF, :], y[1][:, :, VECTOR_SHARE:HALF])
         finish(0)
         finish(1)
-        for q in range(4):
-            eng = nc.scalar if q % 2 == 0 else nc.sync
-            eng.dma_start(
-                out=out_2[0, 4 * q : 4 * q + 4, :].bitcast(I32),
-                in_=y_plane[32 * q : 32 * q + 4, :].bitcast(I32),
-            )
+        for q in range(QUADRANTS):
+            parts, rows = plane_rows(q)
+            queue = nc.scalar if q % 2 == 0 else nc.sync
+            queue.dma_start(out=out_2[0, rows, :].bitcast(I32), in_=y_plane[parts, :].bitcast(I32))

from contextlib import ExitStack

import concourse.mybir as mybir

F32 = mybir.dt.float32
BF16 = mybir.dt.bfloat16
I32 = mybir.dt.int32
U32 = mybir.dt.uint32
U16 = mybir.dt.uint16
U8 = mybir.dt.uint8
FP8X4 = mybir.dt.float8_e4m3fn_x4
TANH = mybir.ActivationFunctionType.Tanh
MULT = mybir.AluOpType.mult
ADD = mybir.AluOpType.add

P = 128
PACK = 4
PAIRS = PACK // 2
QUADRANTS = 4
K = 512
ROWS = 512
COLS = 512
TABLE = 1024
HALF = COLS // 2
LIST_ROWS = 16
RUN = 4
VECTOR_SHARE = 160
FLOPS = 4 * 2 * K * ROWS * COLS


def tile_picked_zcft_tanh_po_kernel(
    tc, x_words, x_scales, eT, w1, w2, w3, w4, dec, offs, out_0, out_1, out_2
):
    nc = tc.nc
    with ExitStack() as ctx:
        keep = ctx.enter_context(tc.tile_pool(name="keep", bufs=1))
        psum = ctx.enter_context(tc.psum_pool(name="psum", bufs=1))

        def sb(name, shape, dtype):
            return keep.tile(shape, dtype, name=name, align_bytes=64)

        def vector_copy(out, in_):
            nc.vector.tensor_copy(out=out, in_=in_)

        def scalar_copy(out, in_):
            nc.scalar.copy(out=out, in_=in_)

        def plane_rows(q):
            return slice(32 * q, 32 * q + 4), slice(4 * q, 4 * q + 4)

        def half(h):
            return slice(h * HALF, (h + 1) * HALF)

        def pair(u):
            return slice(2 * u, 2 * u + 2)

        offsets = keep.tile([P, COLS // LIST_ROWS], U16, name="offsets")
        nc.sync.dma_start(offsets[:], offs)

        table_words = sb("table_words", [P, TABLE], U32)
        nc.sync.dma_start(
            out=table_words[:].bitcast(I32),
            in_=x_words[0].rearrange("p c r -> p (c r)").bitcast(I32),
        )
        table_plane = sb("table_plane", [P, TABLE], U8)
        nc.vector.memset(table_plane[:].bitcast(I32), 0)
        for q in range(QUADRANTS):
            parts, rows = plane_rows(q)
            nc.sync.dma_start(out=table_plane[parts, :].bitcast(I32), in_=x_scales[0, rows, :].bitcast(I32))

        def load(name, src):
            raw = sb(name, [P, PACK, src.shape[1]], F32)
            nc.sync.dma_start(out=raw[:], in_=src.rearrange("(p j) c -> p j c", j=PACK))
            return raw

        e_raw = load("e_raw", eT)
        w2_raw = load("w2_raw", w2)
        w1_raw = load("w1_raw", w1)
        w3_raw = load("w3_raw", w3)
        w4_raw = load("w4_raw", w4)
        dec_rows = dec.rearrange("(p t) c -> p t c", t=PACK)
        dec_sb = []
        for u in range(PAIRS):
            dec_pair = sb("dec%d" % u, [P, 2, COLS], F32)
            nc.sync.dma_start(out=dec_pair[:], in_=dec_rows[:, pair(u), :])
            dec_sb.append(dec_pair)

        x_codes = sb("x_codes", [P, COLS], U32)
        x_plane = sb("x_plane", [P, COLS], U8)
        nc.vector.tensor_copy(out=x_codes[:], in_=table_words[:].indirect(offsets[:]))
        nc.vector.tensor_copy(out=x_plane[:], in_=table_plane[:].indirect(offsets[:]))

        def interleave(copy, grouped, rows):
            copy(
                grouped.rearrange("p (c i) t -> p c t i", i=RUN),
                rows.rearrange("p t (c i) -> p c t i", i=RUN),
            )

        def quantize(codes, plane, grouped):
            nc.vector.quantize_mx(out=codes.bitcast(FP8X4), scales=plane, in_=grouped)

        shared = (vector_copy, scalar_copy)
        e_codes = sb("e_codes", [P, COLS], U32)
        e_plane = sb("e_plane", [P, COLS], U8)
        e_bf = [sb("e_bf%d" % h, [P, HALF, PACK], BF16) for h in range(2)]
        for h, copy in enumerate(shared):
            interleave(copy, e_bf[h][:], e_raw[:, :, half(h)])
        for h in range(2):
            quantize(e_codes[:, half(h)], e_plane[:, half(h)], e_bf[h][:].rearrange("p c t -> p (c t)"))

        def weight_pass(name, raw, copies, banks, rhs_codes, rhs_plane, first):
            dealt = raw[:].rearrange("p j (m t) -> p m j t", t=PACK)
            bf = [sb("%s_bf%d" % (name, u), [P, 2, P, PACK], BF16) for u in range(PAIRS)]
            for u in range(PAIRS):
                copies[u](bf[u][:].rearrange("p t m j -> p m j t"), dealt[:, :, :, pair(u)])
            for u in range(PAIRS):
                codes = sb("%s_codes%d" % (name, u), [P, 2 * P], U32)
                plane = sb("%s_plane%d" % (name, u), [P, 2 * P], U8)
                quantize(codes[:], plane[:], bf[u][:].rearrange("p t m j -> p (t m j)"))
                for s in range(2):
                    nc.tensor.matmul_mx(
                        out=banks[2 * u + s][:],
                        lhsT=codes[:, s * P : (s + 1) * P].bitcast(FP8X4),
                        lhsT_scale=plane[:, s * P : (s + 1) * P],
                        rhs=rhs_codes[:].bitcast(FP8X4),
                        rhs_scale=rhs_plane[:],
                        start=first,
                        stop=not first,
                    )

        g_banks = [psum.tile([P, COLS], F32, name="g_bank%d" % t) for t in range(PACK)]
        h_banks = [psum.tile([P, COLS], F32, name="h_bank%d" % t) for t in range(PACK)]
        weight_pass("w2", w2_raw, shared, g_banks, x_codes, x_plane, True)
        weight_pass("w1", w1_raw, shared, g_banks, e_codes, e_plane, False)
        g_sb = [sb("g%d" % u, [P, 2, COLS], F32) for u in range(PAIRS)]
        for t in range(PACK):
            nc.scalar.activation(out=g_sb[t // 2][:, t % 2, :], in_=g_banks[t][:], func=TANH)
        weight_pass("w3", w3_raw, (vector_copy, vector_copy), h_banks, e_codes, e_plane, True)
        weight_pass("w4", w4_raw, shared, h_banks, x_codes, x_plane, False)

        scaled = [[sb("scaled%d_%d" % (h, u), [P, 2, HALF], F32) for u in range(PAIRS)] for h in range(2)]
        y = [sb("y%d" % h, [P, PACK, HALF], F32) for h in range(2)]
        y_bf = [sb("y_bf%d" % h, [P, HALF, PACK], BF16) for h in range(2)]
        y_codes = sb("y_codes", [P, COLS], U32)
        y_plane = sb("y_plane", [P, COLS], U8)
        out_rows = out_0.rearrange("(p t) c -> p t c", t=PACK)
        out_words = out_1[0].rearrange("p c r -> p (c r)").bitcast(I32)

        def scale(h, u):
            nc.vector.tensor_tensor(
                out=scaled[h][u][:], in0=dec_sb[u][:, :, half(h)], in1=g_sb[u][:, :, half(h)], op=MULT
            )

        def shift(h, u):
            for s in range(2):
                nc.vector.tensor_tensor(
                    out=y[h][:, 2 * u + s, :], in0=h_banks[2 * u + s][:, half(h)], in1=scaled[h][u][:, s, :], op=ADD
                )
            nc.sync.dma_start(out=out_rows[:, pair(u), half(h)], in_=y[h][:, pair(u), :])

        def finish(h):
            quantize(y_codes[:, half(h)], y_plane[:, half(h)], y_bf[h][:].rearrange("p c t -> p (c t)"))
            nc.sync.dma_start(out=out_words[:, half(h)], in_=y_codes[:, half(h)].bitcast(I32))

        scale(0, 0)
        shift(0, 0)
        scale(0, 1)
        scale(1, 0)
        shift(0, 1)
        interleave(scalar_copy, y_bf[0][:], y[0][:])
        scale(1, 1)
        shift(1, 0)
        shift(1, 1)
        interleave(vector_copy, y_bf[1][:, 0:VECTOR_SHARE, :], y[1][:, :, 0:VECTOR_SHARE])
        interleave(scalar_copy, y_bf[1][:, VECTOR_SHARE:HALF, :], y[1][:, :, VECTOR_SHARE:HALF])
        finish(0)
        finish(1)
        for q in range(QUADRANTS):
            parts, rows = plane_rows(q)
            queue = nc.scalar if q % 2 == 0 else nc.sync
            queue.dma_start(out=out_2[0, rows, :].bitcast(I32), in_=y_plane[parts, :].bitcast(I32))
